import numpy as np
import ml_dtypes


def mxq(x, axis, fmt="e4m3"):
    dtype, down = {"e4m3": (ml_dtypes.float8_e4m3fn, 7), "e5m2": (ml_dtypes.float8_e5m2, 14)}[fmt]
    v = np.moveaxis(np.asarray(x, np.float32).astype(ml_dtypes.bfloat16).astype(np.float64), axis, -1)
    blocks = v.reshape(v.shape[:-1] + (-1, 32))
    amax = np.abs(blocks).max(-1, keepdims=True)
    byte = np.maximum(np.where(amax > 0, np.frexp(amax)[1] - 1 + 127, 0) - down, 1)
    scale = np.exp2(byte - 127.0)
    codes = (blocks / scale).astype(np.float32).astype(dtype).astype(np.float64)
    return np.moveaxis((codes * scale).reshape(v.shape), -1, axis)


WIDE = False


def mx_kscale(k):
    if not WIDE:
        return np.ones(k)
    levels = np.array([30, -30])
    if k % 512:
        return np.exp2(np.random.permutation(np.resize(levels, k // 32))).repeat(32)
    a = np.empty((k // 512, 16))
    for p in range(k // 512):
        a[p, :8] = np.random.permutation(np.resize(levels, 8))
        for g in range(8):
            far = levels[np.abs(levels - a[p, g]) >= 10]
            a[p, g + 8] = far[np.random.randint(len(far))]
    return np.exp2(a.ravel()).repeat(32)


def f64(x):
    return np.asarray(x).astype(np.float64)


def striped(idx):
    return np.tile(np.asarray(idx).reshape(-1, 16).T, (8, 1)).astype(np.uint16)


def unstriped(offs):
    return offs[:16].T.reshape(-1).astype(np.int64)


E2M1 = np.array([0.0, 0.5, 1.0, 1.5, 2.0, 3.0, 4.0, 6.0, -0.0, -0.5, -1.0, -1.5, -2.0, -3.0, -4.0, -6.0])


def pack_weight(w, fmt):
    k, n = w.shape
    w = f64(np.asarray(w, np.float32).astype(ml_dtypes.bfloat16)).reshape(k // 32, 32, n)
    amax = np.abs(w).max(1)
    if fmt in ("e4m3", "e5m2"):
        byte = np.frexp(amax)[1] - 1 + 127 - (7 if fmt == "e4m3" else 14)
    else:
        mant, ex = np.frexp(amax / 6.0)
        byte = np.where(mant > 0.5, ex, ex - 1) + 127
    byte = np.clip(np.where(amax > 0, byte, 1), 1, 254)
    scaled = (w * np.exp2(127.0 - byte)[:, None, :]).reshape(k, n).astype(np.float32)
    by_word = np.ascontiguousarray(scaled.reshape(k // 512, 128, 4, n).transpose(0, 1, 3, 2))
    if fmt in ("e4m3", "e5m2"):
        words = by_word.astype(ml_dtypes.float8_e4m3fn if fmt == "e4m3" else ml_dtypes.float8_e5m2).view(np.uint8)
    else:
        c = by_word.astype(ml_dtypes.float4_e2m1fn).view(np.uint8) & 0xF
        words = (c[..., 0::2] | (c[..., 1::2] << 4)).reshape(k // 512, 128, 2 * n)
    return np.ascontiguousarray(words), np.ascontiguousarray(byte.astype(np.uint8).reshape(k // 512, 16, n))


def unpack_weight(words, scales, fmt):
    g, _, n = scales.shape
    words = np.ascontiguousarray(words).reshape(g, 128, n, -1)
    if fmt in ("e4m3", "e5m2"):
        vals = words.view(ml_dtypes.float8_e4m3fn if fmt == "e4m3" else ml_dtypes.float8_e5m2).astype(np.float64)
    else:
        nib = np.empty((g, 128, n, 4), np.uint8)
        nib[..., 0::2] = words & 0xF
        nib[..., 1::2] = words >> 4
        vals = E2M1[nib]
    vals = vals * np.repeat(np.exp2(scales.astype(np.float64) - 127.0), 8, axis=1)[..., None]
    return vals.transpose(0, 1, 3, 2).reshape(g * 512, n)


K, T, J, R, V, M, Q, O, U, X, D, N, E = 512, 1024, 256, 512, 1024, 512, 128, 64, 64, 128, 256, 256, 512


def setup_inputs():
    n = np.random.standard_normal
    idx = np.random.permutation(V)[:R]
    idx2 = np.random.permutation(T)[:J]
    idx3 = np.random.permutation(J)[:O]
    idx4 = np.random.permutation(J)[:U]
    idx5 = np.random.permutation(T)[:D]
    idx6 = np.random.permutation(E)[:D]
    idx7 = np.random.permutation(E)[:D]
    fk = mx_kscale(K)
    fm = mx_kscale(M)
    fr = mx_kscale(R)
    xtp = pack_weight(n((K, T)) / fk[:, None], "e2m1")
    wtp = pack_weight(n((K, V)) * 1 / np.sqrt(K) * fk[:, None], "e5m2")
    xcp = pack_weight(n((M, Q)) / fm[:, None], "e4m3")
    wgp = pack_weight(n((M, R)) * 1 / np.sqrt(M) * fm[:, None] * fr, "e2m1")
    wbp = pack_weight(n((R, N)) * 1 / np.sqrt(R) / fr[:, None], "e4m3")
    wsp = pack_weight(n((K, N)) * 1 / np.sqrt(K) * fk[:, None], "e4m3")
    return {
        "xt_words": xtp[0],
        "xt_scales": xtp[1],
        "wt_words": wtp[0],
        "wt_scales": wtp[1],
        "xc_words": xcp[0],
        "xc_scales": xcp[1],
        "wg_words": wgp[0],
        "wg_scales": wgp[1],
        "wb_words": wbp[0],
        "wb_scales": wbp[1],
        "ws_words": wsp[0],
        "ws_scales": wsp[1],
        "offs": striped(idx),
        "offs2": striped(idx2),
        "offs3": striped(idx3),
        "offs4": striped(idx4),
        "offs5": striped(idx5),
        "offs6": striped(idx6),
        "offs7": striped(idx7),
    }


def reference(xt_words, xt_scales, wt_words, wt_scales, xc_words, xc_scales, wg_words, wg_scales, wb_words, wb_scales, ws_words, ws_scales, offs, offs2, offs3, offs4, offs5, offs6, offs7):
    idx = unstriped(offs)
    idx2 = unstriped(offs2)
    idx3 = unstriped(offs3)
    idx4 = unstriped(offs4)
    idx5 = unstriped(offs5)
    idx6 = unstriped(offs6)
    idx7 = unstriped(offs7)
    xtu = unpack_weight(xt_words, xt_scales, "e2m1")
    wtu = unpack_weight(wt_words, wt_scales, "e5m2")
    xcu = unpack_weight(xc_words, xc_scales, "e4m3")
    wgu = unpack_weight(wg_words, wg_scales, "e2m1")
    wbu = unpack_weight(wb_words, wb_scales, "e4m3")
    wsu = unpack_weight(ws_words, ws_scales, "e4m3")
    wtidxg = wtu[:, idx]
    xtidx2g = xtu[:, idx2]
    a = wtidxg.T @ xtidx2g
    g0 = wgu.T @ xcu
    ga = g0[:, 0:1]
    gb = g0[:, 64:65]
    h1 = a[:, idx3] * ga
    h2 = a[:, idx4] * gb
    h3 = np.concatenate([h1, h2], axis=1)
    hid = np.concatenate([h3, g0], axis=1)
    hidq = mxq(hid, 0, "e5m2")
    xtidx5g = xtu[:, idx5]
    p = wbu.T @ hidq + wsu.T @ xtidx5g
    pa = np.zeros((N, E))
    pa[:, idx6] = p
    pb = np.zeros((N, E))
    pb[:, idx7] = p
    y = pa + pb
    return y

@@ -1,0 +1,211 @@
+from contextlib import ExitStack
+
+import concourse.mybir as mybir
+from concourse.masks import make_identity
+
+K, T, J, R, V, M, Q, O, U, X, D, N, E = 512, 1024, 256, 512, 1024, 512, 128, 64, 64, 128, 256, 256, 512
+FLOPS = 2 * (K * R * J + M * R * Q + R * N * D + K * N * D)
+
+F32 = mybir.dt.float32
+BF16 = mybir.dt.bfloat16
+I32 = mybir.dt.int32
+U32 = mybir.dt.uint32
+U16 = mybir.dt.uint16
+U8 = mybir.dt.uint8
+E4M3 = mybir.dt.float8_e4m3fn_x4
+E5M2 = mybir.dt.float8_e5m2_x4
+E2M1 = mybir.dt.float4_e2m1fn_x4
+COPY = mybir.ActivationFunctionType.Copy
+ADD = mybir.AluOpType.add
+
+P = 128
+PACK = 4
+QUAD = 32
+PER_COL = 16
+
+
+def tile_list_ctxthirds_chosen_further_pagetwice_kernel(
+    tc, xt_words, xt_scales, wt_words, wt_scales, xc_words, xc_scales, wg_words, wg_scales,
+    wb_words, wb_scales, ws_words, ws_scales, offs, offs2, offs3, offs4, offs5, offs6, offs7, out,
+):
+    nc = tc.nc
+    with ExitStack() as ctx:
+        sb = ctx.enter_context(tc.tile_pool(name="sb", bufs=1))
+        ps = ctx.enter_context(tc.psum_pool(name="ps", bufs=1))
+
+        def load_list(src, name):
+            tile = sb.tile(list(src.shape), U16, name=name)
+            nc.sync.dma_start(tile[:], src)
+            return tile
+
+        def load_words(src, cols, dtype, name):
+            tile = sb.tile([P, cols], dtype, name=name, align_bytes=64)
+            rows = src[0] if src.ndim == 3 else src[0].rearrange("p c r -> p (c r)")
+            nc.sync.dma_start(tile[:].bitcast(I32), rows.bitcast(I32))
+            return tile
+
+        def zeroed_plane(cols, name):
+            tile = sb.tile([P, cols], U8, name=name, align_bytes=64)
+            nc.vector.memset(tile[:].bitcast(I32), 0)
+            return tile
+
+        def load_plane_by_quadrant(tile, src):
+            for quad in range(4):
+                nc.sync.dma_start(
+                    tile[QUAD * quad : QUAD * quad + 4, :].bitcast(I32), src[0, 4 * quad : 4 * quad + 4, :].bitcast(I32)
+                )
+
+        def stage_scales(stage, c0, src):
+            cols = src.shape[2]
+            nc.sync.dma_start(
+                stage[0:4, :, c0 // 4 : (c0 + cols) // 4], src[0].bitcast(I32).rearrange("(q r) c -> r q c", r=4)
+            )
+
+        def spread(plane, stage):
+            for quad in range(4):
+                nc.vector.tensor_copy(plane[QUAD * quad : QUAD * quad + 4, :].bitcast(I32), stage[0:4, quad, :])
+
+        wt_plane = zeroed_plane(V, "wt_plane")
+        xt_plane = zeroed_plane(T, "xt_plane")
+        ctx_plane = zeroed_plane(R + Q, "ctx_plane")
+        out_plane = zeroed_plane(2 * N, "out_plane")
+        pages = [[sb.tile([P, E], F32, name="page%d%d" % (s, h)) for h in range(2)] for s in range(2)]
+        for s in range(2):
+            for h in range(2):
+                nc.vector.memset(pages[s][h][:], 0.0)
+        ident = sb.tile([P, P], F32, name="ident")
+        make_identity(nc, ident[:])
+
+        ctx_stage = sb.tile([4, 4, (R + Q) // 4], I32, name="ctx_stage")
+        stage_scales(ctx_stage, 0, wg_scales)
+        stage_scales(ctx_stage, R, xc_scales)
+        xc_w = load_words(xc_words, Q, U32, "xc_w")
+        wg_w = load_words(wg_words, R, U16, "wg_w")
+        l2 = load_list(offs2, "l2")
+        xt_w = load_words(xt_words, T, U16, "xt_w")
+        l1 = load_list(offs, "l1")
+        wt_w = load_words(wt_words, V, U32, "wt_w")
+        load_plane_by_quadrant(wt_plane, wt_scales)
+        load_plane_by_quadrant(xt_plane, xt_scales)
+        l3 = load_list(offs3, "l3")
+        l4 = load_list(offs4, "l4")
+        l5 = load_list(offs5, "l5")
+        out_stage = sb.tile([4, 4, 2 * N // 4], I32, name="out_stage")
+        stage_scales(out_stage, 0, wb_scales)
+        stage_scales(out_stage, N, ws_scales)
+        wb_w = load_words(wb_words, N, U32, "wb_w")
+        ws_w = load_words(ws_words, N, U32, "ws_w")
+        l6 = load_list(offs6, "l6")
+        l7 = load_list(offs7, "l7")
+
+        spread(ctx_plane, ctx_stage)
+        g0t_ps = ps.tile([P, R], F32, name="g0t_ps", tag="bank_g0t")
+        nc.tensor.matmul_mx(g0t_ps[:], lhsT=xc_w[:].bitcast(E4M3), lhsT_scale=ctx_plane[:, R : R + Q],
+                            rhs=wg_w[:].bitcast(E2M1), rhs_scale=ctx_plane[:, 0:R], start=True, stop=True)
+        g0t = sb.tile([P, PACK, P], F32, name="g0t")
+        nc.scalar.activation(g0t[:], g0t_ps[:].rearrange("q (p t) -> q t p", t=PACK), COPY)
+        g0_ps = ps.tile([P, PACK, Q], F32, name="g0_ps")
+        for t in range(PACK):
+            nc.tensor.transpose(g0_ps[:, t, :], g0t[:, t, :], ident[:])
+        gains = sb.tile([P, PACK, 2], F32, name="gains")
+        nc.scalar.activation(gains[:], g0_ps[:, :, 0:Q:64], COPY)
+        hid_g = sb.tile([P, Q, PACK], BF16, name="hid_g", align_bytes=64)
+        nc.scalar.activation(hid_g[:], g0_ps[:].rearrange("p t q -> p q t"), COPY)
+
+        wt_gw = sb.tile([P, R], U32, name="wt_gw", align_bytes=64)
+        wt_gs = sb.tile([P, R], U8, name="wt_gs", align_bytes=64)
+        x2_w = sb.tile([P, J], U16, name="x2_w", align_bytes=64)
+        x2_s = sb.tile([P, J], U8, name="x2_s", align_bytes=64)
+        nc.vector.tensor_copy(x2_w[:], xt_w[:].indirect(l2[:]))
+        nc.vector.tensor_copy(wt_gw[:].rearrange("p (t q) -> p q t", t=PACK), wt_w[:].indirect(l1[:]))
+        nc.vector.tensor_copy(wt_gs[:].rearrange("p (t q) -> p q t", t=PACK), wt_plane[:].indirect(l1[:]))
+        nc.vector.tensor_copy(x2_s[:], xt_plane[:].indirect(l2[:]))
+
+        def gather_tokens(offsets, cols, name):
+            words = sb.tile([P, cols], U16, name=name + "_w", align_bytes=64)
+            scales = sb.tile([P, cols], U8, name=name + "_s", align_bytes=64)
+            nc.vector.tensor_copy(words[:], xt_w[:].indirect(offsets))
+            nc.vector.tensor_copy(scales[:], xt_plane[:].indirect(offsets))
+            return words, scales
+
+        a_ps = [ps.tile([P, J], F32, name="a_ps%d" % t) for t in range(PACK)]
+        for t in range(PACK):
+            cols = slice(P * t, P * (t + 1))
+            nc.tensor.matmul_mx(a_ps[t][:], lhsT=wt_gw[:, cols].bitcast(E5M2), lhsT_scale=wt_gs[:, cols],
+                                rhs=x2_w[:].bitcast(E2M1), rhs_scale=x2_s[:], start=True, stop=True)
+
+        def quantise(hid, name):
+            codes = sb.tile([P, X], U32, name=name + "_w", align_bytes=64)
+            scales = sb.tile([P, X], U8, name=name + "_s", align_bytes=64)
+            nc.vector.quantize_mx(codes[:].bitcast(E5M2), scales[:], hid[:].rearrange("p c t -> p (c t)"))
+            return codes, scales
+
+        def short_way(acc, h, tokens):
+            nc.tensor.matmul_mx(acc, lhsT=ws_w[:, P * h : P * (h + 1)].bitcast(E4M3),
+                                lhsT_scale=out_plane[:, N + P * h : N + P * (h + 1)],
+                                rhs=tokens[0][:].bitcast(E2M1), rhs_scale=tokens[1][:], start=True, stop=False)
+
+        def long_way(acc, h, hidq):
+            nc.tensor.matmul_mx(acc, lhsT=wb_w[:, P * h : P * (h + 1)].bitcast(E4M3),
+                                lhsT_scale=out_plane[:, P * h : P * (h + 1)],
+                                rhs=hidq[0][:].bitcast(E5M2), rhs_scale=hidq[1][:], start=False, stop=True)
+
+        half = X // PER_COL
+        a = [sb.tile([P, J], F32, name="a%d" % t) for t in range(PACK)]
+        h3 = sb.tile([P, 2, PACK, O], F32, name="h3")
+        for t in range(PACK):
+            if t % 2 == 0:
+                nc.scalar.activation(a[t][:], a_ps[t][:], COPY)
+            else:
+                nc.vector.tensor_copy(a[t][:], a_ps[t][:])
+            for s, lst in enumerate((l3, l4)):
+                nc.scalar.activation(h3[:, s, t, :], a[t][:].indirect(lst[:]), COPY, scale=gains[:, t, s : s + 1])
+
+        spread(out_plane, out_stage)
+        x5_g = gather_tokens(l5[:, half : 2 * half], X, "x5_g")
+        hidq_g = quantise(hid_g, "hidq_g")
+        pg_ps = ps.tile([P, 2, X], F32, name="pg_ps")
+        for h in range(2):
+            short_way(pg_ps[:, h, :], h, x5_g)
+            long_way(pg_ps[:, h, :], h, hidq_g)
+        x5_p = gather_tokens(l5[:, 0:half], X, "x5_p")
+        pp_ps = [ps.tile([P, X], F32, name="pp_ps0", tag="bank_g0t"), ps.tile([P, X], F32, name="pp_ps1")]
+        for h in range(2):
+            short_way(pp_ps[h][:], h, x5_p)
+        pg = sb.tile([P, 2, X], F32, name="pg")
+        nc.vector.tensor_copy(pg[:], pg_ps[:])
+
+        hid_p = sb.tile([P, X, PACK], BF16, name="hid_p", align_bytes=64)
+        for s in range(2):
+            nc.vector.tensor_copy(hid_p[:, O * s : O * (s + 1), :], h3[:, s, :, :].rearrange("p t c -> p c t"))
+        hidq_p = quantise(hid_p, "hidq_p")
+        pp = [sb.tile([P, X], F32, name="pp%d" % h) for h in range(2)]
+        for h in range(2):
+            long_way(pp_ps[h][:], h, hidq_p)
+
+        def on_vector(page, offsets, values):
+            nc.vector.tensor_copy(page[:].indirect(offsets), values)
+
+        def on_scalar(page, offsets, values):
+            nc.scalar.activation(page[:].indirect(offsets), values, COPY)
+
+        early = slice(half, 2 * half)
+        late = slice(0, half)
+        y = [sb.tile([P, E], F32, name="y%d" % h) for h in range(2)]
+
+        def finish(h):
+            nc.vector.tensor_tensor(y[h][:], pages[0][h][:], pages[1][h][:], ADD)
+            nc.sync.dma_start(out[P * h : P * (h + 1), :], y[h][:])
+
+        on_scalar(pages[1][0], l7[:, early], pg[:, 0, :])
+        on_vector(pages[0][0], l6[:, early], pg[:, 0, :])
+        nc.vector.tensor_copy(pp[0][:], pp_ps[0][:])
+        nc.vector.tensor_copy(pp[1][:], pp_ps[1][:])
+        on_scalar(pages[1][1], l7[:, early], pg[:, 1, :])
+        on_vector(pages[0][0], l6[:, late], pp[0][:])
+        on_scalar(pages[1][0], l7[:, late], pp[0][:])
+        on_vector(pages[0][1], l6[:, late], pp[1][:])
+        on_scalar(pages[0][1], l6[:, early], pg[:, 1, :])
+        finish(0)
+        on_scalar(pages[1][1], l7[:, late], pp[1][:])
+        finish(1)

@@ -38,14 +38,14 @@ def tile_list_ctxthirds_chosen_further_pagetwice_kernel(
             nc.sync.dma_start(tile[:], src)
             return tile
 
-        def load_words(src, cols, dtype, name):
+        def load_words(src, cols, dtype, name, queue):
             tile = sb.tile([P, cols], dtype, name=name, align_bytes=64)
             rows = src[0] if src.ndim == 3 else src[0].rearrange("p c r -> p (c r)")
-            nc.sync.dma_start(tile[:].bitcast(I32), rows.bitcast(I32))
+            queue.dma_start(tile[:].bitcast(I32), rows.bitcast(I32))
             return tile
 
         def zeroed_plane(cols, name):
-            tile = sb.tile([P, cols], U8, name=name, align_bytes=64)
+            tile = sb.tile([P, cols], U8, name=name, tag=name, align_bytes=64)
             nc.vector.memset(tile[:].bitcast(I32), 0)
             return tile
 
@@ -65,46 +65,46 @@ def tile_list_ctxthirds_chosen_further_pagetwice_kernel(
             for quad in range(4):
                 nc.vector.tensor_copy(plane[QUAD * quad : QUAD * quad + 4, :].bitcast(I32), stage[0:4, quad, :])
 
-        wt_plane = zeroed_plane(V, "wt_plane")
         xt_plane = zeroed_plane(T, "xt_plane")
-        ctx_plane = zeroed_plane(R + Q, "ctx_plane")
-        out_plane = zeroed_plane(2 * N, "out_plane")
+        wt_plane = zeroed_plane(V, "wt_plane")
+        plain_plane = zeroed_plane(R + Q + 2 * N, "plain_plane")
+        ctx_plane = plain_plane[:, 0 : R + Q]
+        out_plane = plain_plane[:, R + Q : R + Q + 2 * N]
         pages = [[sb.tile([P, E], F32, name="page%d%d" % (s, h)) for h in range(2)] for s in range(2)]
         for s in range(2):
             for h in range(2):
                 nc.vector.memset(pages[s][h][:], 0.0)
+
+        wg_w = load_words(wg_words, R, U16, "wg_w", nc.gpsimd)
+        xt_w = load_words(xt_words, T, U16, "xt_w", nc.gpsimd)
         ident = sb.tile([P, P], F32, name="ident")
         make_identity(nc, ident[:])
-
-        ctx_stage = sb.tile([4, 4, (R + Q) // 4], I32, name="ctx_stage")
-        stage_scales(ctx_stage, 0, wg_scales)
-        stage_scales(ctx_stage, R, xc_scales)
-        xc_w = load_words(xc_words, Q, U32, "xc_w")
-        wg_w = load_words(wg_words, R, U16, "wg_w")
-        l2 = load_list(offs2, "l2")
-        xt_w = load_words(xt_words, T, U16, "xt_w")
+        stage = sb.tile([4, 4, (R + Q + 2 * N) // 4], I32, name="stage")
+        stage_scales(stage, 0, wg_scales)
+        stage_scales(stage, R, xc_scales)
+        stage_scales(stage, R + Q, wb_scales)
+        stage_scales(stage, R + Q + N, ws_scales)
         l1 = load_list(offs, "l1")
-        wt_w = load_words(wt_words, V, U32, "wt_w")
-        load_plane_by_quadrant(wt_plane, wt_scales)
+        wt_w = load_words(wt_words, V, U32, "wt_w", nc.sync)
+        xc_w = load_words(xc_words, Q, U32, "xc_w", nc.sync)
+        l2 = load_list(offs2, "l2")
         load_plane_by_quadrant(xt_plane, xt_scales)
+        load_plane_by_quadrant(wt_plane, wt_scales)
+        l5 = load_list(offs5, "l5")
         l3 = load_list(offs3, "l3")
         l4 = load_list(offs4, "l4")
-        l5 = load_list(offs5, "l5")
-        out_stage = sb.tile([4, 4, 2 * N // 4], I32, name="out_stage")
-        stage_scales(out_stage, 0, wb_scales)
-        stage_scales(out_stage, N, ws_scales)
-        wb_w = load_words(wb_words, N, U32, "wb_w")
-        ws_w = load_words(ws_words, N, U32, "ws_w")
+        wb_w = load_words(wb_words, N, U32, "wb_w", nc.sync)
+        ws_w = load_words(ws_words, N, U32, "ws_w", nc.sync)
         l6 = load_list(offs6, "l6")
         l7 = load_list(offs7, "l7")
 
-        spread(ctx_plane, ctx_stage)
+        spread(plain_plane, stage)
         g0t_ps = ps.tile([P, R], F32, name="g0t_ps", tag="bank_g0t")
         nc.tensor.matmul_mx(g0t_ps[:], lhsT=xc_w[:].bitcast(E4M3), lhsT_scale=ctx_plane[:, R : R + Q],
                             rhs=wg_w[:].bitcast(E2M1), rhs_scale=ctx_plane[:, 0:R], start=True, stop=True)
         g0t = sb.tile([P, PACK, P], F32, name="g0t")
         nc.scalar.activation(g0t[:], g0t_ps[:].rearrange("q (p t) -> q t p", t=PACK), COPY)
-        g0_ps = ps.tile([P, PACK, Q], F32, name="g0_ps")
+        g0_ps = ps.tile([P, PACK, Q], F32, name="g0_ps", tag="bank_g0")
         for t in range(PACK):
             nc.tensor.transpose(g0_ps[:, t, :], g0t[:, t, :], ident[:])
         gains = sb.tile([P, PACK, 2], F32, name="gains")
@@ -116,10 +116,10 @@ def tile_list_ctxthirds_chosen_further_pagetwice_kernel(
         wt_gs = sb.tile([P, R], U8, name="wt_gs", align_bytes=64)
         x2_w = sb.tile([P, J], U16, name="x2_w", align_bytes=64)
         x2_s = sb.tile([P, J], U8, name="x2_s", align_bytes=64)
-        nc.vector.tensor_copy(x2_w[:], xt_w[:].indirect(l2[:]))
         nc.vector.tensor_copy(wt_gw[:].rearrange("p (t q) -> p q t", t=PACK), wt_w[:].indirect(l1[:]))
-        nc.vector.tensor_copy(wt_gs[:].rearrange("p (t q) -> p q t", t=PACK), wt_plane[:].indirect(l1[:]))
         nc.vector.tensor_copy(x2_s[:], xt_plane[:].indirect(l2[:]))
+        nc.vector.tensor_copy(x2_w[:], xt_w[:].indirect(l2[:]))
+        nc.vector.tensor_copy(wt_gs[:].rearrange("p (t q) -> p q t", t=PACK), wt_plane[:].indirect(l1[:]))
 
         def gather_tokens(offsets, cols, name):
             words = sb.tile([P, cols], U16, name=name + "_w", align_bytes=64)
@@ -128,14 +128,26 @@ def tile_list_ctxthirds_chosen_further_pagetwice_kernel(
             nc.vector.tensor_copy(scales[:], xt_plane[:].indirect(offsets))
             return words, scales
 
-        a_ps = [ps.tile([P, J], F32, name="a_ps%d" % t) for t in range(PACK)]
-        for t in range(PACK):
+        def slots(acc, t):
             cols = slice(P * t, P * (t + 1))
-            nc.tensor.matmul_mx(a_ps[t][:], lhsT=wt_gw[:, cols].bitcast(E5M2), lhsT_scale=wt_gs[:, cols],
+            nc.tensor.matmul_mx(acc, lhsT=wt_gw[:, cols].bitcast(E5M2), lhsT_scale=wt_gs[:, cols],
                                 rhs=x2_w[:].bitcast(E2M1), rhs_scale=x2_s[:], start=True, stop=True)
 
-        def quantise(hid, name):
-            codes = sb.tile([P, X], U32, name=name + "_w", align_bytes=64)
+        a = [sb.tile([P, J], F32, name="a%d" % t, tag="a%d" % t) for t in range(PACK)]
+        h3 = sb.tile([P, 2, PACK, O], F32, name="h3", tag="h3")
+
+        a0_ps = ps.tile([P, J], F32, name="a0_ps", tag="bank_g0t")
+        slots(a0_ps[:], 0)
+        a12_ps = ps.tile([P, 2, J], F32, name="a12_ps", tag="bank_g0")
+        slots(a12_ps[:, 0, :], 1)
+        slots(a12_ps[:, 1, :], 2)
+        nc.scalar.activation(a[0][:], a0_ps[:], COPY)
+        a3_ps = ps.tile([P, J], F32, name="a3_ps", tag="bank_g0t")
+        slots(a3_ps[:], 3)
+        nc.scalar.activation(a[1][:], a12_ps[:, 0, :], COPY)
+
+        def quantise(hid, name, tag):
+            codes = sb.tile([P, X], U32, name=name + "_w", tag=tag, align_bytes=64)
             scales = sb.tile([P, X], U8, name=name + "_s", align_bytes=64)
             nc.vector.quantize_mx(codes[:].bitcast(E5M2), scales[:], hid[:].rearrange("p c t -> p (c t)"))
             return codes, scales
@@ -151,37 +163,8 @@ def tile_list_ctxthirds_chosen_further_pagetwice_kernel(
                                 rhs=hidq[0][:].bitcast(E5M2), rhs_scale=hidq[1][:], start=False, stop=True)
 
         half = X // PER_COL
-        a = [sb.tile([P, J], F32, name="a%d" % t) for t in range(PACK)]
-        h3 = sb.tile([P, 2, PACK, O], F32, name="h3")
-        for t in range(PACK):
-            if t % 2 == 0:
-                nc.scalar.activation(a[t][:], a_ps[t][:], COPY)
-            else:
-                nc.vector.tensor_copy(a[t][:], a_ps[t][:])
-            for s, lst in enumerate((l3, l4)):
-                nc.scalar.activation(h3[:, s, t, :], a[t][:].indirect(lst[:]), COPY, scale=gains[:, t, s : s + 1])
-
-        spread(out_plane, out_stage)
-        x5_g = gather_tokens(l5[:, half : 2 * half], X, "x5_g")
-        hidq_g = quantise(hid_g, "hidq_g")
-        pg_ps = ps.tile([P, 2, X], F32, name="pg_ps")
-        for h in range(2):
-            short_way(pg_ps[:, h, :], h, x5_g)
-            long_way(pg_ps[:, h, :], h, hidq_g)
-        x5_p = gather_tokens(l5[:, 0:half], X, "x5_p")
-        pp_ps = [ps.tile([P, X], F32, name="pp_ps0", tag="bank_g0t"), ps.tile([P, X], F32, name="pp_ps1")]
-        for h in range(2):
-            short_way(pp_ps[h][:], h, x5_p)
-        pg = sb.tile([P, 2, X], F32, name="pg")
-        nc.vector.tensor_copy(pg[:], pg_ps[:])
-
-        hid_p = sb.tile([P, X, PACK], BF16, name="hid_p", align_bytes=64)
-        for s in range(2):
-            nc.vector.tensor_copy(hid_p[:, O * s : O * (s + 1), :], h3[:, s, :, :].rearrange("p t c -> p c t"))
-        hidq_p = quantise(hid_p, "hidq_p")
-        pp = [sb.tile([P, X], F32, name="pp%d" % h) for h in range(2)]
-        for h in range(2):
-            long_way(pp_ps[h][:], h, hidq_p)
+        early = slice(half, 2 * half)
+        late = slice(0, half)
 
         def on_vector(page, offsets, values):
             nc.vector.tensor_copy(page[:].indirect(offsets), values)
@@ -189,23 +172,56 @@ def tile_list_ctxthirds_chosen_further_pagetwice_kernel(
         def on_scalar(page, offsets, values):
             nc.scalar.activation(page[:].indirect(offsets), values, COPY)
 
-        early = slice(half, 2 * half)
-        late = slice(0, half)
+        x5_g = gather_tokens(l5[:, early], X, "x5_g")
+        hidq_g = quantise(hid_g, "hidq_g", "wt_plane")
+        pg_ps = ps.tile([P, 2, X], F32, name="pg_ps")
+        for h in range(2):
+            short_way(pg_ps[:, h, :], h, x5_g)
+            long_way(pg_ps[:, h, :], h, hidq_g)
+        x5_p = gather_tokens(l5[:, late], X, "x5_p")
+
+        nc.vector.tensor_copy(a[2][:], a12_ps[:, 1, :])
+        nc.vector.tensor_copy(a[3][:], a3_ps[:])
+        for t, s in ((0, 0), (0, 1), (1, 0), (1, 1), (2, 0), (3, 0), (2, 1), (3, 1)):
+            nc.scalar.activation(h3[:, s, t, :], a[t][:].indirect((l3, l4)[s][:]), COPY, scale=gains[:, t, s : s + 1])
+
+        pg_v1 = sb.tile([P, X // 2], F32, name="pg_v1", tag="turns", align_bytes=64)
+        nc.vector.tensor_copy(pg_v1[:], pg_ps[:, 1, 0 : X // 2])
+        on_vector(pages[0][1], l6[:, half : half + half // 2], pg_v1[:])
+
+        pg_s = sb.tile([P, 2, X], F32, name="pg_s", tag="a%d" % (PACK - 1))
+        nc.scalar.activation(pg_s[:], pg_ps[:], COPY)
+
+        hid_p = sb.tile([P, X, PACK], BF16, name="hid_p", tag="turns", align_bytes=64)
+        for s in range(2):
+            nc.vector.tensor_copy(hid_p[:, O * s : O * (s + 1), :], h3[:, s, :, :].rearrange("p t c -> p c t"))
+        pg_v0 = sb.tile([P, X], F32, name="pg_v0", tag="h3")
+        nc.vector.tensor_copy(pg_v0[:], pg_ps[:, 0, :])
+        hidq_p = quantise(hid_p, "hidq_p", "hidq_p_w")
+        pp_ps = [ps.tile([P, X], F32, name="pp_ps0"), ps.tile([P, X], F32, name="pp_ps1")]
+        pp = [sb.tile([P, X], F32, name="pp%d" % h) for h in range(2)]
+        for h in range(2):
+            short_way(pp_ps[h][:], h, x5_p)
+        for h in range(2):
+            long_way(pp_ps[h][:], h, hidq_p)
+
+        for h in range(2):
+            on_scalar(pages[1][h], l7[:, early], pg_s[:, h, :])
+        on_vector(pages[0][0], l6[:, early], pg_v0[:])
+
         y = [sb.tile([P, E], F32, name="y%d" % h) for h in range(2)]
 
         def finish(h):
-            nc.vector.tensor_tensor(y[h][:], pages[0][h][:], pages[1][h][:], ADD)
-            nc.sync.dma_start(out[P * h : P * (h + 1), :], y[h][:])
+            for c in range(2):
+                cols = slice(c * E // 2, (c + 1) * E // 2)
+                nc.vector.tensor_tensor(y[h][:, cols], pages[0][h][:, cols], pages[1][h][:, cols], ADD)
+                nc.sync.dma_start(out[P * h : P * (h + 1), cols], y[h][:, cols])
 
-        on_scalar(pages[1][0], l7[:, early], pg[:, 0, :])
-        on_vector(pages[0][0], l6[:, early], pg[:, 0, :])
-        nc.vector.tensor_copy(pp[0][:], pp_ps[0][:])
-        nc.vector.tensor_copy(pp[1][:], pp_ps[1][:])
-        on_scalar(pages[1][1], l7[:, early], pg[:, 1, :])
-        on_vector(pages[0][0], l6[:, late], pp[0][:])
-        on_scalar(pages[1][0], l7[:, late], pp[0][:])
-        on_vector(pages[0][1], l6[:, late], pp[1][:])
-        on_scalar(pages[0][1], l6[:, early], pg[:, 1, :])
+        for h in range(2):
+            nc.vector.tensor_copy(pp[h][:], pp_ps[h][:])
+        for h in range(2):
+            on_vector(pages[0][h], l6[:, late], pp[h][:])
+            on_scalar(pages[1][h], l7[:, late], pp[h][:])
+        on_scalar(pages[0][1], l6[:, half + half // 2 : 2 * half], pg_s[:, 1, X // 2 : X])
         finish(0)
-        on_scalar(pages[1][1], l7[:, late], pp[1][:])
         finish(1)

from contextlib import ExitStack

import concourse.mybir as mybir
from concourse.masks import make_identity

K, T, J, R, V, M, Q, O, U, X, D, N, E = 512, 1024, 256, 512, 1024, 512, 128, 64, 64, 128, 256, 256, 512
FLOPS = 2 * (K * R * J + M * R * Q + R * N * D + K * N * D)

F32 = mybir.dt.float32
BF16 = mybir.dt.bfloat16
I32 = mybir.dt.int32
U32 = mybir.dt.uint32
U16 = mybir.dt.uint16
U8 = mybir.dt.uint8
E4M3 = mybir.dt.float8_e4m3fn_x4
E5M2 = mybir.dt.float8_e5m2_x4
E2M1 = mybir.dt.float4_e2m1fn_x4
COPY = mybir.ActivationFunctionType.Copy
ADD = mybir.AluOpType.add

P = 128
PACK = 4
QUAD = 32
PER_COL = 16


def tile_list_ctxthirds_chosen_further_pagetwice_kernel(
    tc, xt_words, xt_scales, wt_words, wt_scales, xc_words, xc_scales, wg_words, wg_scales,
    wb_words, wb_scales, ws_words, ws_scales, offs, offs2, offs3, offs4, offs5, offs6, offs7, out,
):
    nc = tc.nc
    with ExitStack() as ctx:
        sb = ctx.enter_context(tc.tile_pool(name="sb", bufs=1))
        ps = ctx.enter_context(tc.psum_pool(name="ps", bufs=1))

        def load_list(src, name):
            tile = sb.tile(list(src.shape), U16, name=name)
            nc.sync.dma_start(tile[:], src)
            return tile

        def load_words(src, cols, dtype, name, queue):
            tile = sb.tile([P, cols], dtype, name=name, align_bytes=64)
            rows = src[0] if src.ndim == 3 else src[0].rearrange("p c r -> p (c r)")
            queue.dma_start(tile[:].bitcast(I32), rows.bitcast(I32))
            return tile

        def zeroed_plane(cols, name):
            tile = sb.tile([P, cols], U8, name=name, tag=name, align_bytes=64)
            nc.vector.memset(tile[:].bitcast(I32), 0)
            return tile

        def load_plane_by_quadrant(tile, src):
            for quad in range(4):
                nc.sync.dma_start(
                    tile[QUAD * quad : QUAD * quad + 4, :].bitcast(I32), src[0, 4 * quad : 4 * quad + 4, :].bitcast(I32)
                )

        def stage_scales(stage, c0, src):
            cols = src.shape[2]
            nc.sync.dma_start(
                stage[0:4, :, c0 // 4 : (c0 + cols) // 4], src[0].bitcast(I32).rearrange("(q r) c -> r q c", r=4)
            )

        def spread(plane, stage):
            for quad in range(4):
                nc.vector.tensor_copy(plane[QUAD * quad : QUAD * quad + 4, :].bitcast(I32), stage[0:4, quad, :])

        xt_plane = zeroed_plane(T, "xt_plane")
        wt_plane = zeroed_plane(V, "wt_plane")
        plain_plane = zeroed_plane(R + Q + 2 * N, "plain_plane")
        ctx_plane = plain_plane[:, 0 : R + Q]
        out_plane = plain_plane[:, R + Q : R + Q + 2 * N]
        pages = [[sb.tile([P, E], F32, name="page%d%d" % (s, h)) for h in range(2)] for s in range(2)]
        for s in range(2):
            for h in range(2):
                nc.vector.memset(pages[s][h][:], 0.0)

        wg_w = load_words(wg_words, R, U16, "wg_w", nc.gpsimd)
        xt_w = load_words(xt_words, T, U16, "xt_w", nc.gpsimd)
        ident = sb.tile([P, P], F32, name="ident")
        make_identity(nc, ident[:])
        stage = sb.tile([4, 4, (R + Q + 2 * N) // 4], I32, name="stage")
        stage_scales(stage, 0, wg_scales)
        stage_scales(stage, R, xc_scales)
        stage_scales(stage, R + Q, wb_scales)
        stage_scales(stage, R + Q + N, ws_scales)
        l1 = load_list(offs, "l1")
        wt_w = load_words(wt_words, V, U32, "wt_w", nc.sync)
        xc_w = load_words(xc_words, Q, U32, "xc_w", nc.sync)
        l2 = load_list(offs2, "l2")
        load_plane_by_quadrant(xt_plane, xt_scales)
        load_plane_by_quadrant(wt_plane, wt_scales)
        l5 = load_list(offs5, "l5")
        l3 = load_list(offs3, "l3")
        l4 = load_list(offs4, "l4")
        wb_w = load_words(wb_words, N, U32, "wb_w", nc.sync)
        ws_w = load_words(ws_words, N, U32, "ws_w", nc.sync)
        l6 = load_list(offs6, "l6")
        l7 = load_list(offs7, "l7")

        spread(plain_plane, stage)
        g0t_ps = ps.tile([P, R], F32, name="g0t_ps", tag="bank_g0t")
        nc.tensor.matmul_mx(g0t_ps[:], lhsT=xc_w[:].bitcast(E4M3), lhsT_scale=ctx_plane[:, R : R + Q],
                            rhs=wg_w[:].bitcast(E2M1), rhs_scale=ctx_plane[:, 0:R], start=True, stop=True)
        g0t = sb.tile([P, PACK, P], F32, name="g0t")
        nc.scalar.activation(g0t[:], g0t_ps[:].rearrange("q (p t) -> q t p", t=PACK), COPY)
        g0_ps = ps.tile([P, PACK, Q], F32, name="g0_ps", tag="bank_g0")
        for t in range(PACK):
            nc.tensor.transpose(g0_ps[:, t, :], g0t[:, t, :], ident[:])
        gains = sb.tile([P, PACK, 2], F32, name="gains")
        nc.scalar.activation(gains[:], g0_ps[:, :, 0:Q:64], COPY)
        hid_g = sb.tile([P, Q, PACK], BF16, name="hid_g", align_bytes=64)
        nc.scalar.activation(hid_g[:], g0_ps[:].rearrange("p t q -> p q t"), COPY)

        wt_gw = sb.tile([P, R], U32, name="wt_gw", align_bytes=64)
        wt_gs = sb.tile([P, R], U8, name="wt_gs", align_bytes=64)
        x2_w = sb.tile([P, J], U16, name="x2_w", align_bytes=64)
        x2_s = sb.tile([P, J], U8, name="x2_s", align_bytes=64)
        nc.vector.tensor_copy(wt_gw[:].rearrange("p (t q) -> p q t", t=PACK), wt_w[:].indirect(l1[:]))
        nc.vector.tensor_copy(x2_s[:], xt_plane[:].indirect(l2[:]))
        nc.vector.tensor_copy(x2_w[:], xt_w[:].indirect(l2[:]))
        nc.vector.tensor_copy(wt_gs[:].rearrange("p (t q) -> p q t", t=PACK), wt_plane[:].indirect(l1[:]))

        def gather_tokens(offsets, cols, name):
            words = sb.tile([P, cols], U16, name=name + "_w", align_bytes=64)
            scales = sb.tile([P, cols], U8, name=name + "_s", align_bytes=64)
            nc.vector.tensor_copy(words[:], xt_w[:].indirect(offsets))
            nc.vector.tensor_copy(scales[:], xt_plane[:].indirect(offsets))
            return words, scales

        def slots(acc, t):
            cols = slice(P * t, P * (t + 1))
            nc.tensor.matmul_mx(acc, lhsT=wt_gw[:, cols].bitcast(E5M2), lhsT_scale=wt_gs[:, cols],
                                rhs=x2_w[:].bitcast(E2M1), rhs_scale=x2_s[:], start=True, stop=True)

        a = [sb.tile([P, J], F32, name="a%d" % t, tag="a%d" % t) for t in range(PACK)]
        h3 = sb.tile([P, 2, PACK, O], F32, name="h3", tag="h3")

        a0_ps = ps.tile([P, J], F32, name="a0_ps", tag="bank_g0t")
        slots(a0_ps[:], 0)
        a12_ps = ps.tile([P, 2, J], F32, name="a12_ps", tag="bank_g0")
        slots(a12_ps[:, 0, :], 1)
        slots(a12_ps[:, 1, :], 2)
        nc.scalar.activation(a[0][:], a0_ps[:], COPY)
        a3_ps = ps.tile([P, J], F32, name="a3_ps", tag="bank_g0t")
        slots(a3_ps[:], 3)
        nc.scalar.activation(a[1][:], a12_ps[:, 0, :], COPY)

        def quantise(hid, name, tag):
            codes = sb.tile([P, X], U32, name=name + "_w", tag=tag, align_bytes=64)
            scales = sb.tile([P, X], U8, name=name + "_s", align_bytes=64)
            nc.vector.quantize_mx(codes[:].bitcast(E5M2), scales[:], hid[:].rearrange("p c t -> p (c t)"))
            return codes, scales

        def short_way(acc, h, tokens):
            nc.tensor.matmul_mx(acc, lhsT=ws_w[:, P * h : P * (h + 1)].bitcast(E4M3),
                                lhsT_scale=out_plane[:, N + P * h : N + P * (h + 1)],
                                rhs=tokens[0][:].bitcast(E2M1), rhs_scale=tokens[1][:], start=True, stop=False)

        def long_way(acc, h, hidq):
            nc.tensor.matmul_mx(acc, lhsT=wb_w[:, P * h : P * (h + 1)].bitcast(E4M3),
                                lhsT_scale=out_plane[:, P * h : P * (h + 1)],
                                rhs=hidq[0][:].bitcast(E5M2), rhs_scale=hidq[1][:], start=False, stop=True)

        half = X // PER_COL
        early = slice(half, 2 * half)
        late = slice(0, half)

        def on_vector(page, offsets, values):
            nc.vector.tensor_copy(page[:].indirect(offsets), values)

        def on_scalar(page, offsets, values):
            nc.scalar.activation(page[:].indirect(offsets), values, COPY)

        x5_g = gather_tokens(l5[:, early], X, "x5_g")
        hidq_g = quantise(hid_g, "hidq_g", "wt_plane")
        pg_ps = ps.tile([P, 2, X], F32, name="pg_ps")
        for h in range(2):
            short_way(pg_ps[:, h, :], h, x5_g)
            long_way(pg_ps[:, h, :], h, hidq_g)
        x5_p = gather_tokens(l5[:, late], X, "x5_p")

        nc.vector.tensor_copy(a[2][:], a12_ps[:, 1, :])
        nc.vector.tensor_copy(a[3][:], a3_ps[:])
        for t, s in ((0, 0), (0, 1), (1, 0), (1, 1), (2, 0), (3, 0), (2, 1), (3, 1)):
            nc.scalar.activation(h3[:, s, t, :], a[t][:].indirect((l3, l4)[s][:]), COPY, scale=gains[:, t, s : s + 1])

        pg_v1 = sb.tile([P, X // 2], F32, name="pg_v1", tag="turns", align_bytes=64)
        nc.vector.tensor_copy(pg_v1[:], pg_ps[:, 1, 0 : X // 2])
        on_vector(pages[0][1], l6[:, half : half + half // 2], pg_v1[:])

        pg_s = sb.tile([P, 2, X], F32, name="pg_s", tag="a%d" % (PACK - 1))
        nc.scalar.activation(pg_s[:], pg_ps[:], COPY)

        hid_p = sb.tile([P, X, PACK], BF16, name="hid_p", tag="turns", align_bytes=64)
        for s in range(2):
            nc.vector.tensor_copy(hid_p[:, O * s : O * (s + 1), :], h3[:, s, :, :].rearrange("p t c -> p c t"))
        pg_v0 = sb.tile([P, X], F32, name="pg_v0", tag="h3")
        nc.vector.tensor_copy(pg_v0[:], pg_ps[:, 0, :])
        hidq_p = quantise(hid_p, "hidq_p", "hidq_p_w")
        pp_ps = [ps.tile([P, X], F32, name="pp_ps0"), ps.tile([P, X], F32, name="pp_ps1")]
        pp = [sb.tile([P, X], F32, name="pp%d" % h) for h in range(2)]
        for h in range(2):
            short_way(pp_ps[h][:], h, x5_p)
        for h in range(2):
            long_way(pp_ps[h][:], h, hidq_p)

        for h in range(2):
            on_scalar(pages[1][h], l7[:, early], pg_s[:, h, :])
        on_vector(pages[0][0], l6[:, early], pg_v0[:])

        y = [sb.tile([P, E], F32, name="y%d" % h) for h in range(2)]

        def finish(h):
            for c in range(2):
                cols = slice(c * E // 2, (c + 1) * E // 2)
                nc.vector.tensor_tensor(y[h][:, cols], pages[0][h][:, cols], pages[1][h][:, cols], ADD)
                nc.sync.dma_start(out[P * h : P * (h + 1), cols], y[h][:, cols])

        for h in range(2):
            nc.vector.tensor_copy(pp[h][:], pp_ps[h][:])
        for h in range(2):
            on_vector(pages[0][h], l6[:, late], pp[h][:])
            on_scalar(pages[1][h], l7[:, late], pp[h][:])
        on_scalar(pages[0][1], l6[:, half + half // 2 : 2 * half], pg_s[:, 1, X // 2 : X])
        finish(0)
        finish(1)
